import numpy as np
import ml_dtypes


def mxq(x, axis, fmt="e4m3"):
    dtype, down = {"e4m3": (ml_dtypes.float8_e4m3fn, 7), "e5m2": (ml_dtypes.float8_e5m2, 14)}[fmt]
    v = np.moveaxis(np.asarray(x, np.float32).astype(ml_dtypes.bfloat16).astype(np.float64), axis, -1)
    blocks = v.reshape(v.shape[:-1] + (-1, 32))
    amax = np.abs(blocks).max(-1, keepdims=True)
    byte = np.maximum(np.where(amax > 0, np.frexp(amax)[1] - 1 + 127, 0) - down, 1)
    scale = np.exp2(byte - 127.0)
    codes = (blocks / scale).astype(np.float32).astype(dtype).astype(np.float64)
    return np.moveaxis((codes * scale).reshape(v.shape), -1, axis)


WIDE = False


def mx_kscale(k):
    if not WIDE:
        return np.ones(k)
    levels = np.array([10, -10, 5, -5, 0])
    if k % 512:
        return np.exp2(np.random.permutation(np.resize(levels, k // 32))).repeat(32)
    a = np.empty((k // 512, 16))
    for p in range(k // 512):
        a[p, :8] = np.random.permutation(np.resize(levels, 8))
        for g in range(8):
            far = levels[np.abs(levels - a[p, g]) >= 10]
            a[p, g + 8] = far[np.random.randint(len(far))]
    return np.exp2(a.ravel()).repeat(32)


def f64(x):
    return np.asarray(x).astype(np.float64)


def striped(idx):
    return np.tile(idx.reshape(-1, 16).T, (8, 1)).astype(np.uint16)


def unstriped(offs):
    return offs[:16].T.reshape(-1).astype(np.int64)


def pack_weight(w):
    k, n = w.shape
    w = f64(np.asarray(w, np.float32).astype(ml_dtypes.bfloat16)).reshape(k // 32, 32, n)
    amax = np.abs(w).max(1)
    byte = np.clip(np.where(amax > 0, np.frexp(amax)[1] - 1 + 127 - 7, 1), 1, 254)
    scaled = (w * np.exp2(127.0 - byte)[:, None, :]).reshape(k, n).astype(np.float32)
    words = np.ascontiguousarray(scaled.reshape(k // 512, 128, 4, n).transpose(0, 1, 3, 2)).astype(ml_dtypes.float8_e4m3fn).view(np.uint8)
    return words, np.ascontiguousarray(byte.astype(np.uint8).reshape(k // 512, 16, n))


def unpack_weight(words, scales):
    g, p, n, _ = words.shape
    vals = np.ascontiguousarray(words).view(ml_dtypes.float8_e4m3fn).astype(np.float64) * np.repeat(np.exp2(scales.astype(np.float64) - 127.0), 8, axis=1)[..., None]
    return vals.transpose(0, 1, 3, 2).reshape(g * 512, n)


def relu(v):
    return np.maximum(v, 0.0)


K, T, S, H, V, D, W = 1024, 2048, 512, 512, 512, 4, 2048
P = 2 ** 7


def setup_inputs():
    n = np.random.standard_normal
    s = mx_kscale(K)[:, None]
    u = mx_kscale(H)
    packed_xT = pack_weight(n((K, T)) * s)
    packed_eT = pack_weight(n((H, W)) / np.sqrt(H) / u[:, None])
    return {
        "x_words": packed_xT[0],
        "x_scales": packed_xT[1],
        "w1": (n((K, H)) / np.sqrt(K) / s * u).astype(np.float32),
        "e_words": packed_eT[0],
        "e_scales": packed_eT[1],
        "own": (np.random.uniform(0.8, 1.6, (S, 1))).astype(np.float32),
        "inv": (np.random.uniform(0.6, 1.2, (S, 1))).astype(np.float32),
        "qn": (np.tile(np.random.uniform(0.8, 1.6, W), (P, 1))).astype(np.float32),
        "offs": striped(np.random.permutation(T)[:S]),
        "code": striped(np.random.permutation(W)[:V]),
    }


def reference(x_words, x_scales, w1, e_words, e_scales, own, inv, qn, offs, code):
    xq = unpack_weight(x_words, x_scales)[:, unstriped(offs)]
    h = mxq(f64(w1), 0, "e4m3").T @ xq
    e_code = unpack_weight(e_words, e_scales)[:, unstriped(code)]
    y = 0.4 * ((mxq(h, 0, "e4m3").T @ e_code))
    rr = -1.0 * y + f64(own)
    par = f64(inv) * ((rr) ** 2)
    tot = rr - y + f64(qn)[:1][:, unstriped(code)]
    l = 3.0 * par + relu(tot - par)
    return l.reshape(len(l), -1, D).min(axis=2)

@@ -1,0 +1,209 @@
+from contextlib import ExitStack
+
+import concourse.mybir as mybir
+from concourse.masks import make_identity
+
+K, T, S, H, V, D, W = 1024, 2048, 512, 512, 512, 4, 2048
+FLOPS = 2 * K * H * S + 2 * H * S * V
+
+F32 = mybir.dt.float32
+BF16 = mybir.dt.bfloat16
+I32 = mybir.dt.int32
+U32 = mybir.dt.uint32
+U16 = mybir.dt.uint16
+U8 = mybir.dt.uint8
+FP8X4 = mybir.dt.float8_e4m3fn_x4
+ACT = mybir.ActivationFunctionType
+ALU = mybir.AluOpType
+AXIS = mybir.AxisListType
+
+P = 128
+PACK = 4
+K_PASS = P * PACK
+PASSES = K // K_PASS
+BLOCKS = S // P
+QUADS = 4
+LIST_COLS = P // 16
+
+
+def tile_picked_yscann_min_p_kernel(
+    tc, x_words, x_scales, w1, e_words, e_scales, own, inv, qn, offs, code, out
+):
+    nc = tc.nc
+    with ExitStack() as ctx:
+        sb = ctx.enter_context(tc.tile_pool(name="sb", bufs=1))
+        ps = ctx.enter_context(tc.psum_pool(name="ps", bufs=1))
+
+        def tiles(name, count, shape, dtype):
+            return [sb.tile(shape, dtype, name=name + str_of[i], align_bytes=64) for i in range(count)]
+
+        str_of = ["0", "1", "2", "3"]
+
+        offs_t = sb.tile([P, S // 16], U16, name="offs_t")
+        code_t = sb.tile([P, V // 16], U16, name="code_t")
+        x_scale_table = sb.tile([P, T], U8, name="x_scale_table", align_bytes=64)
+        e_scale_table = sb.tile([P, W], U8, name="e_scale_table", align_bytes=64)
+        x_word_table = tiles("x_word_table", PASSES, [P, T], U32)
+        e_word_table = sb.tile([P, W], U32, name="e_word_table", align_bytes=64)
+        w_raw = tiles("w_raw", PASSES, [P, PACK, H], F32)
+        q_table = sb.tile([P, W], F32, name="q_table", align_bytes=64)
+        rows = sb.tile([P, P], F32, name="rows", align_bytes=64)
+        ident = sb.tile([P, P], F32, name="ident", align_bytes=64)
+
+        nc.gpsimd.memset(rows[:], 0.0)
+        nc.vector.memset(x_scale_table[:].bitcast(I32), 0)
+        nc.vector.memset(e_scale_table[:].bitcast(I32), 0)
+        nc.vector.memset(q_table[:], 0.0)
+
+        def load_words(table, words):
+            nc.sync.dma_start(out=table[:].bitcast(I32), in_=words.rearrange("p n t -> p (n t)").bitcast(I32))
+
+        def load_w(g):
+            nc.sync.dma_start(
+                out=w_raw[g][:], in_=w1[g * K_PASS : (g + 1) * K_PASS, :].rearrange("(p j) c -> p j c", j=PACK)
+            )
+
+        nc.sync.dma_start(offs_t[:], offs)
+        load_w(0)
+        nc.sync.dma_start(code_t[:], code)
+        for q in range(QUADS):
+            nc.scalar.dma_start(
+                out=x_scale_table[32 * q : 32 * q + 4 * PASSES, :].bitcast(I32),
+                in_=x_scales[:, 4 * q : 4 * q + 4, :].bitcast(I32),
+            )
+        load_words(x_word_table[0], x_words[0])
+        load_w(1)
+        load_words(x_word_table[1], x_words[1])
+        load_words(e_word_table, e_words[0])
+        nc.scalar.dma_start(out=q_table[0:1, :], in_=qn[0:1, :])
+        nc.gpsimd.dma_start(out=rows[0:BLOCKS, :], in_=own.rearrange("(b t) o -> b (t o)", b=BLOCKS))
+        nc.gpsimd.dma_start(out=rows[BLOCKS : 2 * BLOCKS, :], in_=inv.rearrange("(b t) o -> b (t o)", b=BLOCKS))
+        for q in range(QUADS):
+            nc.gpsimd.dma_start(
+                out=e_scale_table[32 * q : 32 * q + 4, :].bitcast(I32),
+                in_=e_scales[0, 4 * q : 4 * q + 4, :].bitcast(I32),
+            )
+        make_identity(nc, ident[:])
+
+        x_scale = sb.tile([P, S], U8, name="x_scale", align_bytes=64)
+        e_scale = sb.tile([P, V], U8, name="e_scale", align_bytes=64)
+        x_code = tiles("x_code", PASSES, [P, S], U32)
+        e_code = sb.tile([P, V], U32, name="e_code", align_bytes=64)
+        w_bf = tiles("w_bf", PASSES, [P, PACK * H], BF16)
+        w_code = tiles("w_code", PASSES, [P, H], U32)
+        w_scale = tiles("w_scale", PASSES, [P, H], U8)
+        h_bf = tiles("h_bf", BLOCKS, [P, P * PACK], BF16)
+        h_code = tiles("h_code", BLOCKS, [P, P], U32)
+        h_scale = tiles("h_scale", BLOCKS, [P, P], U8)
+        h_bank = [ps.tile([P, PACK, P], F32, name="h_bank" + str_of[b]) for b in range(BLOCKS)]
+
+        def round_w(g, half):
+            dst = w_bf[g][:].rearrange("p (t m j) -> p m j t", t=PACK, j=PACK)
+            src = w_raw[g][:].rearrange("p j (m t) -> p m j t", t=PACK)
+            nc.vector.tensor_copy(out=dst[:, :half], in_=src[:, :half])
+            if half < P:
+                nc.scalar.copy(out=dst[:, half:], in_=src[:, half:])
+
+        def quantise(codes, scales, values):
+            nc.vector.quantize_mx(out=codes[:].bitcast(FP8X4), scales=scales[:], in_=values[:])
+
+        def first_product(g, b):
+            cols = slice(b * P, (b + 1) * P)
+            for t in range(PACK):
+                w_cols = slice(t * P, (t + 1) * P)
+                nc.tensor.matmul_mx(
+                    out=h_bank[b][:, t, :],
+                    lhsT=w_code[g][:, w_cols].bitcast(FP8X4),
+                    lhsT_scale=w_scale[g][:, w_cols],
+                    rhs=x_code[g][:, cols].bitcast(FP8X4),
+                    rhs_scale=x_scale[4 * g : P, cols],
+                    start=(g == 0 and t == 0),
+                    stop=(g == PASSES - 1 and t == PACK - 1),
+                )
+
+        round_w(0, P)
+        quantise(w_code[0], w_scale[0], w_bf[0])
+        nc.vector.tensor_copy(x_scale[:], x_scale_table[:].indirect(offs_t[:]))
+
+        token_bank = ps.tile([P, V], F32, name="y_bank1")
+        nc.tensor.transpose(token_bank[:, 0:P], rows[:], ident[:])
+        own_col = sb.tile([P, BLOCKS], F32, name="own_col")
+        inv2_col = sb.tile([P, BLOCKS], F32, name="inv2_col")
+        inv3_col = sb.tile([P, BLOCKS], F32, name="inv3_col")
+        nc.scalar.copy(out=own_col[:], in_=token_bank[:, 0:BLOCKS])
+        nc.scalar.activation(inv2_col[:], token_bank[:, BLOCKS : 2 * BLOCKS], ACT.Copy, scale=2.0)
+        nc.scalar.activation(inv3_col[:], token_bank[:, BLOCKS : 2 * BLOCKS], ACT.Copy, scale=3.0)
+
+        nc.vector.tensor_copy(x_code[0][:], x_word_table[0][:].indirect(offs_t[:]))
+        nc.vector.tensor_copy(e_scale[:], e_scale_table[:].indirect(code_t[:]))
+
+        q_picked = sb.tile([P, V], F32, name="q_picked", align_bytes=64)
+        nc.scalar.activation(q_picked[:], q_table[:].indirect(code_t[:]), ACT.Copy)
+        q_turn_bank = ps.tile([P, V // P, P], F32, name="y_bank2")
+        for c in range(V // P):
+            nc.tensor.transpose(q_turn_bank[:, c, :], q_picked[:, c * P : (c + 1) * P], ident[:])
+        q_col = sb.tile([P, V // P], F32, name="q_col")
+        nc.scalar.copy(out=q_col[:], in_=q_turn_bank[:, :, 0])
+        q_bank = ps.tile([P, V], F32, name="y_bank3")
+        for c in range(V // P):
+            nc.tensor.transpose(q_bank[:, c * P : (c + 1) * P], q_col[:, c : c + 1].to_broadcast([P, P]), ident[:])
+
+        for b in range(BLOCKS):
+            first_product(0, b)
+        round_w(1, P // 2)
+        quantise(w_code[1], w_scale[1], w_bf[1])
+
+        q_own = tiles("q_own", BLOCKS, [P, V], F32)
+        for b in range(BLOCKS):
+            nc.scalar.activation(q_own[b][:], q_bank[:], ACT.Identity, bias=own_col[:, b : b + 1])
+
+        for b in range(BLOCKS):
+            nc.vector.tensor_copy(
+                x_code[1][:, b * P : (b + 1) * P],
+                x_word_table[1][:].indirect(offs_t[:, b * LIST_COLS : (b + 1) * LIST_COLS]),
+            )
+            first_product(1, b)
+            nc.scalar.copy(
+                out=h_bf[b][:].rearrange("p (n t) -> p n t", t=PACK), in_=h_bank[b][:].rearrange("p t n -> p n t")
+            )
+        for b in range(BLOCKS):
+            quantise(h_code[b], h_scale[b], h_bf[b])
+
+        nc.vector.tensor_copy(e_code[:], e_word_table[:].indirect(code_t[:]))
+
+        y_bank = [ps.tile([P, V], F32, name="y_bank" + str_of[b]) for b in range(BLOCKS)]
+        sq = tiles("sq", BLOCKS, [P, V], F32)
+        tot = tiles("tot", BLOCKS, [P, V], F32)
+        upper = tiles("upper", BLOCKS, [P, V], F32)
+        cost = tiles("cost", BLOCKS, [P, V], F32)
+        least = tiles("least", BLOCKS, [P, V // D], F32)
+        for b in range(BLOCKS):
+            nc.tensor.matmul_mx(
+                out=y_bank[b][:],
+                lhsT=h_code[b][:].bitcast(FP8X4),
+                lhsT_scale=h_scale[b][:],
+                rhs=e_code[:].bitcast(FP8X4),
+                rhs_scale=e_scale[:],
+                start=True,
+                stop=True,
+            )
+
+        def read_bank(b):
+            nc.vector.scalar_tensor_tensor(tot[b][:], y_bank[b][:], -0.8, q_own[b][:], ALU.mult, ALU.add)
+            nc.scalar.activation(sq[b][:], y_bank[b][:], ACT.Square, bias=own_col[:, b : b + 1], scale=-0.4)
+
+        def add_parallel(b):
+            nc.vector.scalar_tensor_tensor(upper[b][:], sq[b][:], inv2_col[:, b : b + 1], tot[b][:], ALU.mult, ALU.add)
+
+        def take_larger(b):
+            nc.vector.scalar_tensor_tensor(cost[b][:], sq[b][:], inv3_col[:, b : b + 1], upper[b][:], ALU.mult, ALU.max)
+
+        def take_least(b):
+            nc.vector.tensor_reduce(least[b][:], cost[b][:].rearrange("p (g d) -> p g d", d=D), AXIS.X, ALU.min)
+            nc.sync.dma_start(out=out[b * P : (b + 1) * P, :], in_=least[b][:])
+
+        stages = [read_bank, add_parallel, take_larger, take_least]
+        for pair in range(0, BLOCKS, 2):
+            for stage in stages:
+                stage(pair)
+                stage(pair + 1)

@@ -24,6 +24,7 @@ PASSES = K // K_PASS
 BLOCKS = S // P
 QUADS = 4
 LIST_COLS = P // 16
+FOLD = W // P
 
 
 def tile_picked_yscann_min_p_kernel(
@@ -47,13 +48,13 @@ def tile_picked_yscann_min_p_kernel(
         e_word_table = sb.tile([P, W], U32, name="e_word_table", align_bytes=64)
         w_raw = tiles("w_raw", PASSES, [P, PACK, H], F32)
         q_table = sb.tile([P, W], F32, name="q_table", align_bytes=64)
+        q_folded = sb.tile([P, FOLD], F32, name="q_folded", align_bytes=64)
         rows = sb.tile([P, P], F32, name="rows", align_bytes=64)
         ident = sb.tile([P, P], F32, name="ident", align_bytes=64)
 
-        nc.gpsimd.memset(rows[:], 0.0)
-        nc.vector.memset(x_scale_table[:].bitcast(I32), 0)
+        nc.gpsimd.memset(x_scale_table[:].bitcast(I32), 0)
+        nc.vector.memset(rows[:], 0.0)
         nc.vector.memset(e_scale_table[:].bitcast(I32), 0)
-        nc.vector.memset(q_table[:], 0.0)
 
         def load_words(table, words):
             nc.sync.dma_start(out=table[:].bitcast(I32), in_=words.rearrange("p n t -> p (n t)").bitcast(I32))
@@ -63,27 +64,33 @@ def tile_picked_yscann_min_p_kernel(
                 out=w_raw[g][:], in_=w1[g * K_PASS : (g + 1) * K_PASS, :].rearrange("(p j) c -> p j c", j=PACK)
             )
 
-        nc.sync.dma_start(offs_t[:], offs)
-        load_w(0)
-        nc.sync.dma_start(code_t[:], code)
-        for q in range(QUADS):
-            nc.scalar.dma_start(
+        def load_x_scales(q):
+            nc.sync.dma_start(
                 out=x_scale_table[32 * q : 32 * q + 4 * PASSES, :].bitcast(I32),
                 in_=x_scales[:, 4 * q : 4 * q + 4, :].bitcast(I32),
             )
-        load_words(x_word_table[0], x_words[0])
-        load_w(1)
-        load_words(x_word_table[1], x_words[1])
-        load_words(e_word_table, e_words[0])
-        nc.scalar.dma_start(out=q_table[0:1, :], in_=qn[0:1, :])
-        nc.gpsimd.dma_start(out=rows[0:BLOCKS, :], in_=own.rearrange("(b t) o -> b (t o)", b=BLOCKS))
-        nc.gpsimd.dma_start(out=rows[BLOCKS : 2 * BLOCKS, :], in_=inv.rearrange("(b t) o -> b (t o)", b=BLOCKS))
-        for q in range(QUADS):
-            nc.gpsimd.dma_start(
+
+        def load_e_scales(q):
+            nc.sync.dma_start(
                 out=e_scale_table[32 * q : 32 * q + 4, :].bitcast(I32),
                 in_=e_scales[0, 4 * q : 4 * q + 4, :].bitcast(I32),
             )
+
         make_identity(nc, ident[:])
+        nc.gpsimd.dma_start(out=rows[0:BLOCKS, :], in_=own.rearrange("(b t) o -> b (t o)", b=BLOCKS))
+        nc.gpsimd.dma_start(out=rows[BLOCKS : 2 * BLOCKS, :], in_=inv.rearrange("(b t) o -> b (t o)", b=BLOCKS))
+        nc.sync.dma_start(offs_t[:], offs)
+        nc.sync.dma_start(out=q_folded[:], in_=qn[0, :].rearrange("(p j) -> p j", j=FOLD))
+        load_w(0)
+        for q in range(QUADS):
+            load_x_scales(q)
+        load_w(1)
+        nc.sync.dma_start(code_t[:], code)
+        load_words(x_word_table[0], x_words[0])
+        for q in range(QUADS):
+            load_e_scales(q)
+        load_words(x_word_table[1], x_words[1])
+        load_words(e_word_table, e_words[0])
 
         x_scale = sb.tile([P, S], U8, name="x_scale", align_bytes=64)
         e_scale = sb.tile([P, V], U8, name="e_scale", align_bytes=64)
@@ -92,9 +99,9 @@ def tile_picked_yscann_min_p_kernel(
         w_bf = tiles("w_bf", PASSES, [P, PACK * H], BF16)
         w_code = tiles("w_code", PASSES, [P, H], U32)
         w_scale = tiles("w_scale", PASSES, [P, H], U8)
-        h_bf = tiles("h_bf", BLOCKS, [P, P * PACK], BF16)
-        h_code = tiles("h_code", BLOCKS, [P, P], U32)
-        h_scale = tiles("h_scale", BLOCKS, [P, P], U8)
+        h_bf = tiles("h_bf", BLOCKS // 2, [P, 2 * P * PACK], BF16)
+        h_code = tiles("h_code", BLOCKS // 2, [P, 2 * P], U32)
+        h_scale = tiles("h_scale", BLOCKS // 2, [P, 2 * P], U8)
         h_bank = [ps.tile([P, PACK, P], F32, name="h_bank" + str_of[b]) for b in range(BLOCKS)]
 
         def round_w(g, half):
@@ -105,7 +112,7 @@ def tile_picked_yscann_min_p_kernel(
                 nc.scalar.copy(out=dst[:, half:], in_=src[:, half:])
 
         def quantise(codes, scales, values):
-            nc.vector.quantize_mx(out=codes[:].bitcast(FP8X4), scales=scales[:], in_=values[:])
+            nc.vector.quantize_mx(out=codes.bitcast(FP8X4), scales=scales, in_=values)
 
         def first_product(g, b):
             cols = slice(b * P, (b + 1) * P)
@@ -121,11 +128,21 @@ def tile_picked_yscann_min_p_kernel(
                     stop=(g == PASSES - 1 and t == PACK - 1),
                 )
 
-        round_w(0, P)
-        quantise(w_code[0], w_scale[0], w_bf[0])
-        nc.vector.tensor_copy(x_scale[:], x_scale_table[:].indirect(offs_t[:]))
+        for a in range(FOLD // 4):
+            q_bank = ps.tile([P, 4, P], F32, name="y_bank" + str_of[a])
+            for j in range(4):
+                col = 4 * a + j
+                nc.tensor.transpose(q_bank[:, j, :], q_folded[:, col : col + 1].to_broadcast([P, P]), ident[:])
+            nc.scalar.copy(
+                out=q_table[:].rearrange("m (p j) -> m p j", j=FOLD)[:, :, 4 * a : 4 * a + 4],
+                in_=q_bank[:].rearrange("m j p -> m p j"),
+            )
 
-        token_bank = ps.tile([P, V], F32, name="y_bank1")
+        round_w(0, P // 2)
+        nc.vector.tensor_copy(x_scale[:], x_scale_table[:].indirect(offs_t[:]))
+        quantise(w_code[0][:], w_scale[0][:], w_bf[0][:])
+
+        token_bank = ps.tile([P, V], F32, name="y_bank3")
         nc.tensor.transpose(token_bank[:, 0:P], rows[:], ident[:])
         own_col = sb.tile([P, BLOCKS], F32, name="own_col")
         inv2_col = sb.tile([P, BLOCKS], F32, name="inv2_col")
@@ -133,67 +150,85 @@ def tile_picked_yscann_min_p_kernel(
         nc.scalar.copy(out=own_col[:], in_=token_bank[:, 0:BLOCKS])
         nc.scalar.activation(inv2_col[:], token_bank[:, BLOCKS : 2 * BLOCKS], ACT.Copy, scale=2.0)
         nc.scalar.activation(inv3_col[:], token_bank[:, BLOCKS : 2 * BLOCKS], ACT.Copy, scale=3.0)
-
-        nc.vector.tensor_copy(x_code[0][:], x_word_table[0][:].indirect(offs_t[:]))
-        nc.vector.tensor_copy(e_scale[:], e_scale_table[:].indirect(code_t[:]))
-
         q_picked = sb.tile([P, V], F32, name="q_picked", align_bytes=64)
         nc.scalar.activation(q_picked[:], q_table[:].indirect(code_t[:]), ACT.Copy)
-        q_turn_bank = ps.tile([P, V // P, P], F32, name="y_bank2")
-        for c in range(V // P):
-            nc.tensor.transpose(q_turn_bank[:, c, :], q_picked[:, c * P : (c + 1) * P], ident[:])
-        q_col = sb.tile([P, V // P], F32, name="q_col")
-        nc.scalar.copy(out=q_col[:], in_=q_turn_bank[:, :, 0])
-        q_bank = ps.tile([P, V], F32, name="y_bank3")
-        for c in range(V // P):
-            nc.tensor.transpose(q_bank[:, c * P : (c + 1) * P], q_col[:, c : c + 1].to_broadcast([P, P]), ident[:])
-
+        q_own = tiles("q_own", BLOCKS // 2, [P, 2, V], F32)
         for b in range(BLOCKS):
-            first_product(0, b)
-        round_w(1, P // 2)
-        quantise(w_code[1], w_scale[1], w_bf[1])
+            nc.scalar.activation(q_own[b // 2][:, b % 2, :], q_picked[:], ACT.Identity, bias=own_col[:, b : b + 1])
 
-        q_own = tiles("q_own", BLOCKS, [P, V], F32)
-        for b in range(BLOCKS):
-            nc.scalar.activation(q_own[b][:], q_bank[:], ACT.Identity, bias=own_col[:, b : b + 1])
+        round_w(1, P)
+        quantise(w_code[1][:], w_scale[1][:], w_bf[1][:])
 
-        for b in range(BLOCKS):
+        def gather_x(g, b):
             nc.vector.tensor_copy(
-                x_code[1][:, b * P : (b + 1) * P],
-                x_word_table[1][:].indirect(offs_t[:, b * LIST_COLS : (b + 1) * LIST_COLS]),
+                x_code[g][:, b * P : (b + 1) * P],
+                x_word_table[g][:].indirect(offs_t[:, b * LIST_COLS : (b + 1) * LIST_COLS]),
             )
+
+        for b in range(BLOCKS):
+            gather_x(0, b)
+            first_product(0, b)
+        nc.vector.tensor_copy(e_scale[:], e_scale_table[:].indirect(code_t[:]))
+
+        for b in range(BLOCKS):
+            gather_x(1, b)
             first_product(1, b)
             nc.scalar.copy(
-                out=h_bf[b][:].rearrange("p (n t) -> p n t", t=PACK), in_=h_bank[b][:].rearrange("p t n -> p n t")
+                out=h_bf[b // 2][:].rearrange("p (n t) -> p n t", t=PACK)[:, (b % 2) * P : (b % 2 + 1) * P, :],
+                in_=h_bank[b][:].rearrange("p t n -> p n t"),
             )
-        for b in range(BLOCKS):
-            quantise(h_code[b], h_scale[b], h_bf[b])
+        quantise(h_code[0][:], h_scale[0][:], h_bf[0][:])
 
-        nc.vector.tensor_copy(e_code[:], e_word_table[:].indirect(code_t[:]))
-
-        y_bank = [ps.tile([P, V], F32, name="y_bank" + str_of[b]) for b in range(BLOCKS)]
+        HALF = V // 2
+        y_bank = [ps.tile([P, 2, HALF], F32, name="y_bank" + str_of[b]) for b in range(BLOCKS)]
         sq = tiles("sq", BLOCKS, [P, V], F32)
-        tot = tiles("tot", BLOCKS, [P, V], F32)
+        tot = tiles("tot", BLOCKS // 2, [P, 2, V], F32)
         upper = tiles("upper", BLOCKS, [P, V], F32)
         cost = tiles("cost", BLOCKS, [P, V], F32)
         least = tiles("least", BLOCKS, [P, V // D], F32)
-        for b in range(BLOCKS):
+
+        def second_product(dst, b, cols):
+            tokens = slice((b % 2) * P, (b % 2 + 1) * P)
             nc.tensor.matmul_mx(
-                out=y_bank[b][:],
-                lhsT=h_code[b][:].bitcast(FP8X4),
-                lhsT_scale=h_scale[b][:],
-                rhs=e_code[:].bitcast(FP8X4),
-                rhs_scale=e_scale[:],
+                out=dst,
+                lhsT=h_code[b // 2][:, tokens].bitcast(FP8X4),
+                lhsT_scale=h_scale[b // 2][:, tokens],
+                rhs=e_code[:, cols].bitcast(FP8X4),
+                rhs_scale=e_scale[:, cols],
                 start=True,
                 stop=True,
             )
 
-        def read_bank(b):
-            nc.vector.scalar_tensor_tensor(tot[b][:], y_bank[b][:], -0.8, q_own[b][:], ALU.mult, ALU.add)
-            nc.scalar.activation(sq[b][:], y_bank[b][:], ACT.Square, bias=own_col[:, b : b + 1], scale=-0.4)
+        for u in range(2):
+            cols = slice(u * HALF, (u + 1) * HALF)
+            nc.vector.tensor_copy(
+                e_code[:, cols], e_word_table[:].indirect(code_t[:, u * HALF // 16 : (u + 1) * HALF // 16])
+            )
+            for b in range(2):
+                second_product(y_bank[u][:, b, :], b, cols)
+        quantise(h_code[1][:], h_scale[1][:], h_bf[1][:])
+        for b in range(2, BLOCKS):
+            second_product(y_bank[b][:].rearrange("p u n -> p (u n)"), b, slice(0, V))
+
+        for u in range(2):
+            cols = slice(u * HALF, (u + 1) * HALF)
+            nc.vector.scalar_tensor_tensor(
+                tot[0][:, :, cols], y_bank[u][:], -0.8,
+                q_own[0][:, :, cols], ALU.mult, ALU.add,
+            )
+            for b in range(2):
+                nc.scalar.activation(
+                    sq[b][:, cols], y_bank[u][:, b, :], ACT.Square, bias=own_col[:, b : b + 1], scale=-0.4
+                )
+        for b in range(2, BLOCKS):
+            whole = y_bank[b][:].rearrange("p u n -> p (u n)")
+            nc.vector.scalar_tensor_tensor(tot[1][:, b - 2, :], whole, -0.8, q_own[1][:, b - 2, :], ALU.mult, ALU.add)
+            nc.scalar.activation(sq[b][:], whole, ACT.Square, bias=own_col[:, b : b + 1], scale=-0.4)
 
         def add_parallel(b):
-            nc.vector.scalar_tensor_tensor(upper[b][:], sq[b][:], inv2_col[:, b : b + 1], tot[b][:], ALU.mult, ALU.add)
+            nc.vector.scalar_tensor_tensor(
+                upper[b][:], sq[b][:], inv2_col[:, b : b + 1], tot[b // 2][:, b % 2, :], ALU.mult, ALU.add
+            )
 
         def take_larger(b):
             nc.vector.scalar_tensor_tensor(cost[b][:], sq[b][:], inv3_col[:, b : b + 1], upper[b][:], ALU.mult, ALU.max)
@@ -202,7 +237,7 @@ def tile_picked_yscann_min_p_kernel(
             nc.vector.tensor_reduce(least[b][:], cost[b][:].rearrange("p (g d) -> p g d", d=D), AXIS.X, ALU.min)
             nc.sync.dma_start(out=out[b * P : (b + 1) * P, :], in_=least[b][:])
 
-        stages = [read_bank, add_parallel, take_larger, take_least]
+        stages = [add_parallel, take_larger, take_least]
         for pair in range(0, BLOCKS, 2):
             for stage in stages:
                 stage(pair)

@@ -52,8 +52,8 @@ def tile_picked_yscann_min_p_kernel(
         rows = sb.tile([P, P], F32, name="rows", align_bytes=64)
         ident = sb.tile([P, P], F32, name="ident", align_bytes=64)
 
+        nc.gpsimd.memset(rows[:], 0.0)
         nc.gpsimd.memset(x_scale_table[:].bitcast(I32), 0)
-        nc.vector.memset(rows[:], 0.0)
         nc.vector.memset(e_scale_table[:].bitcast(I32), 0)
 
         def load_words(table, words):
@@ -77,10 +77,10 @@ def tile_picked_yscann_min_p_kernel(
             )
 
         make_identity(nc, ident[:])
-        nc.gpsimd.dma_start(out=rows[0:BLOCKS, :], in_=own.rearrange("(b t) o -> b (t o)", b=BLOCKS))
-        nc.gpsimd.dma_start(out=rows[BLOCKS : 2 * BLOCKS, :], in_=inv.rearrange("(b t) o -> b (t o)", b=BLOCKS))
         nc.sync.dma_start(offs_t[:], offs)
         nc.sync.dma_start(out=q_folded[:], in_=qn[0, :].rearrange("(p j) -> p j", j=FOLD))
+        nc.sync.dma_start(out=rows[0:BLOCKS, :], in_=own.rearrange("(b t) o -> b (t o)", b=BLOCKS))
+        nc.sync.dma_start(out=rows[BLOCKS : 2 * BLOCKS, :], in_=inv.rearrange("(b t) o -> b (t o)", b=BLOCKS))
         load_w(0)
         for q in range(QUADS):
             load_x_scales(q)

from contextlib import ExitStack

import concourse.mybir as mybir
from concourse.masks import make_identity

K, T, S, H, V, D, W = 1024, 2048, 512, 512, 512, 4, 2048
FLOPS = 2 * K * H * S + 2 * H * S * V

F32 = mybir.dt.float32
BF16 = mybir.dt.bfloat16
I32 = mybir.dt.int32
U32 = mybir.dt.uint32
U16 = mybir.dt.uint16
U8 = mybir.dt.uint8
FP8X4 = mybir.dt.float8_e4m3fn_x4
ACT = mybir.ActivationFunctionType
ALU = mybir.AluOpType
AXIS = mybir.AxisListType

P = 128
PACK = 4
K_PASS = P * PACK
PASSES = K // K_PASS
BLOCKS = S // P
QUADS = 4
LIST_COLS = P // 16
FOLD = W // P


def tile_picked_yscann_min_p_kernel(
    tc, x_words, x_scales, w1, e_words, e_scales, own, inv, qn, offs, code, out
):
    nc = tc.nc
    with ExitStack() as ctx:
        sb = ctx.enter_context(tc.tile_pool(name="sb", bufs=1))
        ps = ctx.enter_context(tc.psum_pool(name="ps", bufs=1))

        def tiles(name, count, shape, dtype):
            return [sb.tile(shape, dtype, name=name + str_of[i], align_bytes=64) for i in range(count)]

        str_of = ["0", "1", "2", "3"]

        offs_t = sb.tile([P, S // 16], U16, name="offs_t")
        code_t = sb.tile([P, V // 16], U16, name="code_t")
        x_scale_table = sb.tile([P, T], U8, name="x_scale_table", align_bytes=64)
        e_scale_table = sb.tile([P, W], U8, name="e_scale_table", align_bytes=64)
        x_word_table = tiles("x_word_table", PASSES, [P, T], U32)
        e_word_table = sb.tile([P, W], U32, name="e_word_table", align_bytes=64)
        w_raw = tiles("w_raw", PASSES, [P, PACK, H], F32)
        q_table = sb.tile([P, W], F32, name="q_table", align_bytes=64)
        q_folded = sb.tile([P, FOLD], F32, name="q_folded", align_bytes=64)
        rows = sb.tile([P, P], F32, name="rows", align_bytes=64)
        ident = sb.tile([P, P], F32, name="ident", align_bytes=64)

        nc.gpsimd.memset(rows[:], 0.0)
        nc.gpsimd.memset(x_scale_table[:].bitcast(I32), 0)
        nc.vector.memset(e_scale_table[:].bitcast(I32), 0)

        def load_words(table, words):
            nc.sync.dma_start(out=table[:].bitcast(I32), in_=words.rearrange("p n t -> p (n t)").bitcast(I32))

        def load_w(g):
            nc.sync.dma_start(
                out=w_raw[g][:], in_=w1[g * K_PASS : (g + 1) * K_PASS, :].rearrange("(p j) c -> p j c", j=PACK)
            )

        def load_x_scales(q):
            nc.sync.dma_start(
                out=x_scale_table[32 * q : 32 * q + 4 * PASSES, :].bitcast(I32),
                in_=x_scales[:, 4 * q : 4 * q + 4, :].bitcast(I32),
            )

        def load_e_scales(q):
            nc.sync.dma_start(
                out=e_scale_table[32 * q : 32 * q + 4, :].bitcast(I32),
                in_=e_scales[0, 4 * q : 4 * q + 4, :].bitcast(I32),
            )

        make_identity(nc, ident[:])
        nc.sync.dma_start(offs_t[:], offs)
        nc.sync.dma_start(out=q_folded[:], in_=qn[0, :].rearrange("(p j) -> p j", j=FOLD))
        nc.sync.dma_start(out=rows[0:BLOCKS, :], in_=own.rearrange("(b t) o -> b (t o)", b=BLOCKS))
        nc.sync.dma_start(out=rows[BLOCKS : 2 * BLOCKS, :], in_=inv.rearrange("(b t) o -> b (t o)", b=BLOCKS))
        load_w(0)
        for q in range(QUADS):
            load_x_scales(q)
        load_w(1)
        nc.sync.dma_start(code_t[:], code)
        load_words(x_word_table[0], x_words[0])
        for q in range(QUADS):
            load_e_scales(q)
        load_words(x_word_table[1], x_words[1])
        load_words(e_word_table, e_words[0])

        x_scale = sb.tile([P, S], U8, name="x_scale", align_bytes=64)
        e_scale = sb.tile([P, V], U8, name="e_scale", align_bytes=64)
        x_code = tiles("x_code", PASSES, [P, S], U32)
        e_code = sb.tile([P, V], U32, name="e_code", align_bytes=64)
        w_bf = tiles("w_bf", PASSES, [P, PACK * H], BF16)
        w_code = tiles("w_code", PASSES, [P, H], U32)
        w_scale = tiles("w_scale", PASSES, [P, H], U8)
        h_bf = tiles("h_bf", BLOCKS // 2, [P, 2 * P * PACK], BF16)
        h_code = tiles("h_code", BLOCKS // 2, [P, 2 * P], U32)
        h_scale = tiles("h_scale", BLOCKS // 2, [P, 2 * P], U8)
        h_bank = [ps.tile([P, PACK, P], F32, name="h_bank" + str_of[b]) for b in range(BLOCKS)]

        def round_w(g, half):
            dst = w_bf[g][:].rearrange("p (t m j) -> p m j t", t=PACK, j=PACK)
            src = w_raw[g][:].rearrange("p j (m t) -> p m j t", t=PACK)
            nc.vector.tensor_copy(out=dst[:, :half], in_=src[:, :half])
            if half < P:
                nc.scalar.copy(out=dst[:, half:], in_=src[:, half:])

        def quantise(codes, scales, values):
            nc.vector.quantize_mx(out=codes.bitcast(FP8X4), scales=scales, in_=values)

        def first_product(g, b):
            cols = slice(b * P, (b + 1) * P)
            for t in range(PACK):
                w_cols = slice(t * P, (t + 1) * P)
                nc.tensor.matmul_mx(
                    out=h_bank[b][:, t, :],
                    lhsT=w_code[g][:, w_cols].bitcast(FP8X4),
                    lhsT_scale=w_scale[g][:, w_cols],
                    rhs=x_code[g][:, cols].bitcast(FP8X4),
                    rhs_scale=x_scale[4 * g : P, cols],
                    start=(g == 0 and t == 0),
                    stop=(g == PASSES - 1 and t == PACK - 1),
                )

        for a in range(FOLD // 4):
            q_bank = ps.tile([P, 4, P], F32, name="y_bank" + str_of[a])
            for j in range(4):
                col = 4 * a + j
                nc.tensor.transpose(q_bank[:, j, :], q_folded[:, col : col + 1].to_broadcast([P, P]), ident[:])
            nc.scalar.copy(
                out=q_table[:].rearrange("m (p j) -> m p j", j=FOLD)[:, :, 4 * a : 4 * a + 4],
                in_=q_bank[:].rearrange("m j p -> m p j"),
            )

        round_w(0, P // 2)
        nc.vector.tensor_copy(x_scale[:], x_scale_table[:].indirect(offs_t[:]))
        quantise(w_code[0][:], w_scale[0][:], w_bf[0][:])

        token_bank = ps.tile([P, V], F32, name="y_bank3")
        nc.tensor.transpose(token_bank[:, 0:P], rows[:], ident[:])
        own_col = sb.tile([P, BLOCKS], F32, name="own_col")
        inv2_col = sb.tile([P, BLOCKS], F32, name="inv2_col")
        inv3_col = sb.tile([P, BLOCKS], F32, name="inv3_col")
        nc.scalar.copy(out=own_col[:], in_=token_bank[:, 0:BLOCKS])
        nc.scalar.activation(inv2_col[:], token_bank[:, BLOCKS : 2 * BLOCKS], ACT.Copy, scale=2.0)
        nc.scalar.activation(inv3_col[:], token_bank[:, BLOCKS : 2 * BLOCKS], ACT.Copy, scale=3.0)
        q_picked = sb.tile([P, V], F32, name="q_picked", align_bytes=64)
        nc.scalar.activation(q_picked[:], q_table[:].indirect(code_t[:]), ACT.Copy)
        q_own = tiles("q_own", BLOCKS // 2, [P, 2, V], F32)
        for b in range(BLOCKS):
            nc.scalar.activation(q_own[b // 2][:, b % 2, :], q_picked[:], ACT.Identity, bias=own_col[:, b : b + 1])

        round_w(1, P)
        quantise(w_code[1][:], w_scale[1][:], w_bf[1][:])

        def gather_x(g, b):
            nc.vector.tensor_copy(
                x_code[g][:, b * P : (b + 1) * P],
                x_word_table[g][:].indirect(offs_t[:, b * LIST_COLS : (b + 1) * LIST_COLS]),
            )

        for b in range(BLOCKS):
            gather_x(0, b)
            first_product(0, b)
        nc.vector.tensor_copy(e_scale[:], e_scale_table[:].indirect(code_t[:]))

        for b in range(BLOCKS):
            gather_x(1, b)
            first_product(1, b)
            nc.scalar.copy(
                out=h_bf[b // 2][:].rearrange("p (n t) -> p n t", t=PACK)[:, (b % 2) * P : (b % 2 + 1) * P, :],
                in_=h_bank[b][:].rearrange("p t n -> p n t"),
            )
        quantise(h_code[0][:], h_scale[0][:], h_bf[0][:])

        HALF = V // 2
        y_bank = [ps.tile([P, 2, HALF], F32, name="y_bank" + str_of[b]) for b in range(BLOCKS)]
        sq = tiles("sq", BLOCKS, [P, V], F32)
        tot = tiles("tot", BLOCKS // 2, [P, 2, V], F32)
        upper = tiles("upper", BLOCKS, [P, V], F32)
        cost = tiles("cost", BLOCKS, [P, V], F32)
        least = tiles("least", BLOCKS, [P, V // D], F32)

        def second_product(dst, b, cols):
            tokens = slice((b % 2) * P, (b % 2 + 1) * P)
            nc.tensor.matmul_mx(
                out=dst,
                lhsT=h_code[b // 2][:, tokens].bitcast(FP8X4),
                lhsT_scale=h_scale[b // 2][:, tokens],
                rhs=e_code[:, cols].bitcast(FP8X4),
                rhs_scale=e_scale[:, cols],
                start=True,
                stop=True,
            )

        for u in range(2):
            cols = slice(u * HALF, (u + 1) * HALF)
            nc.vector.tensor_copy(
                e_code[:, cols], e_word_table[:].indirect(code_t[:, u * HALF // 16 : (u + 1) * HALF // 16])
            )
            for b in range(2):
                second_product(y_bank[u][:, b, :], b, cols)
        quantise(h_code[1][:], h_scale[1][:], h_bf[1][:])
        for b in range(2, BLOCKS):
            second_product(y_bank[b][:].rearrange("p u n -> p (u n)"), b, slice(0, V))

        for u in range(2):
            cols = slice(u * HALF, (u + 1) * HALF)
            nc.vector.scalar_tensor_tensor(
                tot[0][:, :, cols], y_bank[u][:], -0.8,
                q_own[0][:, :, cols], ALU.mult, ALU.add,
            )
            for b in range(2):
                nc.scalar.activation(
                    sq[b][:, cols], y_bank[u][:, b, :], ACT.Square, bias=own_col[:, b : b + 1], scale=-0.4
                )
        for b in range(2, BLOCKS):
            whole = y_bank[b][:].rearrange("p u n -> p (u n)")
            nc.vector.scalar_tensor_tensor(tot[1][:, b - 2, :], whole, -0.8, q_own[1][:, b - 2, :], ALU.mult, ALU.add)
            nc.scalar.activation(sq[b][:], whole, ACT.Square, bias=own_col[:, b : b + 1], scale=-0.4)

        def add_parallel(b):
            nc.vector.scalar_tensor_tensor(
                upper[b][:], sq[b][:], inv2_col[:, b : b + 1], tot[b // 2][:, b % 2, :], ALU.mult, ALU.add
            )

        def take_larger(b):
            nc.vector.scalar_tensor_tensor(cost[b][:], sq[b][:], inv3_col[:, b : b + 1], upper[b][:], ALU.mult, ALU.max)

        def take_least(b):
            nc.vector.tensor_reduce(least[b][:], cost[b][:].rearrange("p (g d) -> p g d", d=D), AXIS.X, ALU.min)
            nc.sync.dma_start(out=out[b * P : (b + 1) * P, :], in_=least[b][:])

        stages = [add_parallel, take_larger, take_least]
        for pair in range(0, BLOCKS, 2):
            for stage in stages:
                stage(pair)
                stage(pair + 1)
